import numpy as np
import ml_dtypes


def mxq(x, axis, fmt="e4m3"):
    dtype, down = {"e4m3": (ml_dtypes.float8_e4m3fn, 7), "e5m2": (ml_dtypes.float8_e5m2, 14)}[fmt]
    v = np.moveaxis(np.asarray(x, np.float32).astype(ml_dtypes.bfloat16).astype(np.float64), axis, -1)
    blocks = v.reshape(v.shape[:-1] + (-1, 32))
    amax = np.abs(blocks).max(-1, keepdims=True)
    byte = np.maximum(np.where(amax > 0, np.frexp(amax)[1] - 1 + 127, 0) - down, 1)
    scale = np.exp2(byte - 127.0)
    codes = (blocks / scale).astype(np.float32).astype(dtype).astype(np.float64)
    return np.moveaxis((codes * scale).reshape(v.shape), -1, axis)


WIDE = False


def mx_kscale(k):
    if not WIDE:
        return np.ones(k)
    levels = np.array([10, -10, 5, -5, 0])
    if k % 512:
        return np.exp2(np.random.permutation(np.resize(levels, k // 32))).repeat(32)
    a = np.empty((k // 512, 16))
    for p in range(k // 512):
        a[p, :8] = np.random.permutation(np.resize(levels, 8))
        for g in range(8):
            far = levels[np.abs(levels - a[p, g]) >= 10]
            a[p, g + 8] = far[np.random.randint(len(far))]
    return np.exp2(a.ravel()).repeat(32)


def f64(x):
    return np.asarray(x).astype(np.float64)


def striped(idx):
    return np.tile(idx.reshape(-1, 16).T, (8, 1)).astype(np.uint16)


def unstriped(offs):
    return offs[:16].T.reshape(-1).astype(np.int64)


def striped8(idx):
    return np.concatenate([x.reshape(-1, 16).T for x in idx]).astype(np.uint16)


def runs(offs, k):
    lists = np.stack([offs[16 * r : 16 * r + 16].T.reshape(-1) for r in range(8)]).astype(np.int64)
    return lists[np.arange(k) % 512 // 64]


def pack_weight(w):
    k, n = w.shape
    w = f64(np.asarray(w, np.float32).astype(ml_dtypes.bfloat16)).reshape(k // 32, 32, n)
    amax = np.abs(w).max(1)
    byte = np.clip(np.where(amax > 0, np.frexp(amax)[1] - 1 + 127 - 7, 1), 1, 254)
    scaled = (w * np.exp2(127.0 - byte)[:, None, :]).reshape(k, n).astype(np.float32)
    words = np.ascontiguousarray(scaled.reshape(k // 512, 128, 4, n).transpose(0, 1, 3, 2)).astype(ml_dtypes.float8_e4m3fn).view(np.uint8)
    return words, np.ascontiguousarray(byte.astype(np.uint8).reshape(k // 512, 16, n))


def unpack_weight(words, scales):
    g, p, n, _ = words.shape
    vals = np.ascontiguousarray(words).view(ml_dtypes.float8_e4m3fn).astype(np.float64) * np.repeat(np.exp2(scales.astype(np.float64) - 127.0), 8, axis=1)[..., None]
    return vals.transpose(0, 1, 3, 2).reshape(g * 512, n)


def sigmoid(v):
    return 1.0 / (1.0 + np.exp(-np.maximum(v, -700.0)))

def planes(y):
    n, m = y.shape
    v = y.astype(np.float32).astype(ml_dtypes.bfloat16).astype(np.float64).reshape(n // 32, 32, m)
    top = np.abs(v).max(1)
    byte = np.clip(np.where(top > 0, np.frexp(top)[1] - 1 + 127 - 7, 1), 1, 254)
    codes = (v * np.exp2(127.0 - byte)[:, None, :]).reshape(n, m).astype(np.float32).astype(ml_dtypes.float8_e4m3fn).view(np.uint8)
    words = codes.reshape(n // 512, 128, 4, m).transpose(0, 1, 3, 2)
    return np.ascontiguousarray(words), np.ascontiguousarray(byte.astype(np.uint8).reshape(n // 512, 16, m))


K, T, S, H, W = 512, 2048, 512, 512, 256


def setup_inputs():
    n = np.random.standard_normal
    s = mx_kscale(K)[:, None]
    u = mx_kscale(H)
    packed_xT = pack_weight(n((K, T)) * s)
    packed_w1 = pack_weight(n((K, H)) / np.sqrt(K) / s)
    packed_w2 = pack_weight(n((H, H)) / np.sqrt(H) / u[:, None])
    perm = np.stack([np.random.permutation(S) for _ in range(8)])
    return {
        "x_words": packed_xT[0],
        "x_scales": packed_xT[1],
        "w1_words": packed_w1[0],
        "w1_scales": packed_w1[1],
        "gn": (np.random.uniform(0.5, 1.5, (H, 1)) * u[:, None]).astype(np.float32),
        "w2_words": packed_w2[0],
        "w2_scales": packed_w2[1],
        "offs": striped(np.random.permutation(T)[:S]),
        "n1": striped8(np.stack([np.random.permutation(S) for _ in range(8)])),
        "n2": striped8(np.stack([np.random.permutation(S) for _ in range(8)])),
        "n3": striped8(perm[:, :W]),
        "n4": striped8(perm[:, W:]),
        "n5": striped8(np.stack([np.random.permutation(S) for _ in range(8)])),
        "n6": striped8(np.stack([np.random.permutation(S) for _ in range(8)])),
    }


def reference(x_words, x_scales, w1_words, w1_scales, gn, w2_words, w2_scales, offs, n1, n2, n3, n4, n5, n6):
    xq = unpack_weight(x_words, x_scales)[:, unstriped(offs)]
    y = unpack_weight(w1_words, w1_scales).T @ xq
    z = f64(gn) * (y * (sigmoid(y[np.arange(H)[:, None], runs(n1, H)] - (y[np.arange(H)[:, None], runs(n2, H)]))))
    w2q = unpack_weight(w2_words, w2_scales)
    a = w2q.T @ mxq(z, 0, "e4m3")
    pa = y[np.arange(H)[:, None], runs(n3, H)]
    pb = y[np.arange(H)[:, None], runs(n4, H)]
    rb = np.maximum(0.5 * pa, pb)
    ra = pb - pa
    ds = np.zeros((H, S))
    ds[np.arange(H)[:, None], runs(n3, H)] = ra
    dt = ds.copy()
    dt[np.arange(H)[:, None], runs(n4, H)] = rb
    z2 = f64(gn) * dt
    b = w2q.T @ mxq(z2, 0, "e4m3")
    out_0 = a[np.arange(H)[:, None], runs(n5, H)] - (np.tanh(b) * (b[np.arange(H)[:, None], runs(n6, H)]))
    return (out_0,) + planes(out_0)

@@ -1,0 +1,215 @@
+from contextlib import ExitStack
+
+import concourse.mybir as mybir
+
+K, T, S, H, W = 512, 2048, 512, 512, 256
+FLOPS = 3 * 2 * K * H * S
+
+F32 = mybir.dt.float32
+BF16 = mybir.dt.bfloat16
+I32 = mybir.dt.int32
+U32 = mybir.dt.uint32
+U16 = mybir.dt.uint16
+U8 = mybir.dt.uint8
+FP8X4 = mybir.dt.float8_e4m3fn_x4
+ALU = mybir.AluOpType
+ACT = mybir.ActivationFunctionType
+
+P = 128
+PACK = 4
+STRIPE = 16
+HALF = S // 2
+PIECES = ((0, 256), (256, 384), (384, 512))
+
+
+def tile_picked_tiesoftbcmplift_none_po_kernel(
+    tc, x_words, x_scales, w1_words, w1_scales, gn, w2_words, w2_scales, offs, n1, n2, n3, n4, n5, n6, out_0, out_1, out_2
+):
+    nc = tc.nc
+    with ExitStack() as ctx:
+        keep = ctx.enter_context(tc.tile_pool(name="keep", bufs=1))
+        ring = ctx.enter_context(tc.tile_pool(name="ring", bufs=2))
+        psum = ctx.enter_context(tc.psum_pool(name="psum", bufs=8))
+
+        def load_list(src, name):
+            tile = keep.tile(list(src.shape), U16, name=name)
+            nc.sync.dma_start(tile[:], src)
+            return tile
+
+        def load_words(src, name, queue):
+            tile = keep.tile([P, src.shape[2]], I32, name=name, align_bytes=64)
+            queue.dma_start(tile[:], src[0].rearrange("p n t -> p (n t)").bitcast(I32))
+            return tile
+
+        def load_scales(src, name, clear, queues):
+            tile = keep.tile([P, src.shape[2]], U8, name=name, align_bytes=64)
+            clear.memset(tile[:].bitcast(I32), 0)
+            for q, queue in enumerate(queues):
+                queue.dma_start(tile[32 * q : 32 * q + 4, :].bitcast(I32), src[0][4 * q : 4 * q + 4, :].bitcast(I32))
+            return tile
+
+        def deal(src, dtype, name):
+            tile = keep.tile([P, H], dtype, name=name, align_bytes=64)
+            nc.vector.tensor_copy(tile[:].rearrange("p (t m) -> p t m", t=PACK), src[:].rearrange("p (m t) -> p t m", t=PACK))
+            return tile
+
+        def entries(lst, c0, c1):
+            return lst[:, c0 // STRIPE : c1 // STRIPE]
+
+        def product(w_codes, w_bytes, t, codes, scale_bytes):
+            acc = psum.tile([P, codes.shape[1]], F32, name="acc")
+            cols = slice(t * P, (t + 1) * P)
+            nc.tensor.matmul_mx(
+                out=acc[:],
+                lhsT=w_codes[:, cols].bitcast(FP8X4),
+                lhsT_scale=w_bytes[:, cols],
+                rhs=codes.bitcast(FP8X4),
+                rhs_scale=scale_bytes,
+                start=True,
+                stop=True,
+            )
+            return acc
+
+        def interleave(copy, rows, name):
+            width = rows.shape[2]
+            tile = keep.tile([P, width, PACK], BF16, name=name, align_bytes=64)
+            copy(tile[:].rearrange("p (c i) t -> p c t i", i=4), rows[:].rearrange("p t (c i) -> p c t i", i=4))
+            return tile[:].rearrange("p c t -> p (c t)")
+
+        def quantise(grouped, name):
+            codes = keep.tile([P, S], U32, name=name + "_codes", align_bytes=64)
+            scale_bytes = keep.tile([P, S], U8, name=name + "_bytes", align_bytes=64)
+            nc.vector.quantize_mx(out=codes[:].bitcast(FP8X4), scales=scale_bytes[:], in_=grouped)
+            return codes[:], scale_bytes[:]
+
+        xw = load_words(x_words, "xw", nc.sync)
+        offs_sb = load_list(offs, "offs_sb")
+        n3_sb = load_list(n3, "n3_sb")
+        n4_sb = load_list(n4, "n4_sb")
+        n2_sb = load_list(n2, "n2_sb")
+        n1_sb = load_list(n1, "n1_sb")
+        n6_sb = load_list(n6, "n6_sb")
+        w1w = load_words(w1_words, "w1w", nc.sync)
+        n5_sb = load_list(n5, "n5_sb")
+        xs = load_scales(x_scales, "xs", nc.gpsimd, [nc.scalar] * 4)
+        w1s = load_scales(w1_scales, "w1s", nc.gpsimd, [nc.gpsimd, nc.gpsimd, nc.scalar, nc.scalar])
+        w2s = load_scales(w2_scales, "w2s", nc.vector, [nc.sync] * 4)
+
+        warm = keep.tile([P, 1], F32)
+        nc.vector.memset(warm[:], 0.0)
+        warm2 = keep.tile([P, 1], F32)
+        nc.scalar.activation(warm2[:], warm[:], ACT.Sigmoid)
+
+        x_codes = keep.tile([P, S], U32, align_bytes=64)
+        nc.vector.tensor_copy(x_codes[:], xw[:].bitcast(U32).indirect(offs_sb[:]))
+        w1c = deal(w1w, I32, "w1c")
+        w2w = load_words(w2_words, "w1w", nc.sync)
+        w1b = deal(w1s, U8, "w1b")
+        gain = keep.tile([P, PACK], F32, name="w1s", align_bytes=64)
+        nc.sync.dma_start(gain[:], gn.rearrange("(p t) o -> p (t o)", t=PACK))
+        x_bytes = keep.tile([P, S], U8, align_bytes=64)
+        for c0 in (0, HALF):
+            nc.vector.tensor_copy(x_bytes[:, c0 : c0 + HALF], xs[:].indirect(entries(offs_sb, c0, c0 + HALF)))
+        w2c = deal(w2w, I32, "w2c")
+        w2b = deal(w2s, U8, "w2b")
+
+        y = []
+        for t in range(PACK):
+            y_t = keep.tile([P, S], F32, name=f"y{t}")
+            for c0 in (0, HALF):
+                acc = product(w1c, w1b, t, x_codes[:, c0 : c0 + HALF], x_bytes[:, c0 : c0 + HALF])
+                nc.scalar.copy(y_t[:, c0 : c0 + HALF], acc[:])
+            y.append(y_t)
+
+        z2_rows = keep.tile([P, PACK, S], BF16)
+        neg_pa, pb, rb, dt = {}, {}, {}, {}
+        for s in range(PACK + 1):
+            t, u = s, s - 1
+            if t < PACK:
+                neg_pa[t] = ring.tile([P, W], F32, name="neg_pa")
+                nc.vector.tensor_scalar(neg_pa[t][:], y[t][:].indirect(n3_sb[:]), -1.0, 0.0, op0=ALU.mult, op1=ALU.add)
+            if u >= 0:
+                rb[u] = ring.tile([P, W], F32, name="rb")
+                nc.vector.scalar_tensor_tensor(rb[u][:], neg_pa[u][:], -0.5, pb[u][:], op0=ALU.mult, op1=ALU.max)
+                dt[u] = ring.tile([P, S], F32, name="dt")
+                nc.vector.tensor_tensor(dt[u][:].indirect(n3_sb[:]), pb[u][:], neg_pa[u][:], ALU.add)
+            if t < PACK:
+                pb[t] = ring.tile([P, W], F32, name="pb")
+                nc.vector.tensor_copy(pb[t][:], y[t][:].indirect(n4_sb[:]))
+            if u >= 0:
+                nc.vector.tensor_copy(dt[u][:].indirect(n4_sb[:]), rb[u][:])
+                nc.scalar.activation(z2_rows[:, u, :], dt[u][:], ACT.Copy, scale=gain[:, u : u + 1])
+        z2_grouped = interleave(nc.scalar.copy, z2_rows, "z2_grouped")
+
+        z_rows = keep.tile([P, PACK, S], BF16)
+        b_win = [keep.tile([P, 2 * S], F32, name=f"b_win{t}") for t in range(PACK)]
+        y2, gate, tanh_b = {}, {}, []
+        for s in range(PACK + 2):
+            for c0 in (0, HALF):
+                cols = slice(c0, c0 + HALF)
+                if s < PACK:
+                    if c0 == 0:
+                        y2[s] = ring.tile([P, S], F32, name="y2")
+                    nc.vector.tensor_copy(y2[s][:, cols], y[s][:].indirect(entries(n2_sb, c0, c0 + HALF)))
+                t = s - 1
+                if 0 <= t < PACK:
+                    nc.vector.tensor_tensor(
+                        b_win[t][:, S + c0 : S + c0 + HALF], y[t][:].indirect(entries(n1_sb, c0, c0 + HALF)), y2[t][:, cols], ALU.subtract
+                    )
+            if 0 <= t < PACK:
+                gate[t] = keep.tile([P, S], F32, name=f"gate{t % 2}")
+                nc.scalar.activation(gate[t][:], b_win[t][:, S:], ACT.Sigmoid)
+            u = s - 2
+            if u >= 0:
+                nc.vector.scalar_tensor_tensor(z_rows[:, u, :], gate[u][:], gain[:, u : u + 1], y[u][:], op0=ALU.mult, op1=ALU.mult)
+            if s == 1:
+                z2_codes, z2_bytes = quantise(z2_grouped, "z2")
+                for v in range(PACK):
+                    acc = product(w2c, w2b, v, z2_codes, z2_bytes)
+                    nc.scalar.copy(b_win[v][:, :S], acc[:])
+                    th_t = keep.tile([P, S], F32, name=f"tanh{v}")
+                    nc.scalar.activation(th_t[:], acc[:], ACT.Tanh)
+                    tanh_b.append(th_t)
+        z_grouped = interleave(nc.scalar.copy, z_rows, "z_grouped")
+
+        prod = []
+        for t in range(PACK):
+            if t < 2:
+                p_t = keep.tile([P, S], F32, name=("y3", "gate1")[t])[:]
+            else:
+                if t == 2:
+                    late = keep.tile([P, 2, S], F32, name="z_grouped", align_bytes=64)
+                p_t = late[:, t - 2, :]
+            nc.vector.tensor_tensor(p_t, b_win[t][:].indirect(n6_sb[:]), tanh_b[t][:], ALU.mult)
+            prod.append(p_t)
+            if t == 1:
+                z_codes, z_bytes = quantise(z_grouped, "z")
+                a = []
+                for v in range(PACK):
+                    acc = product(w2c, w2b, v, z_codes, z_bytes)
+                    a_t = keep.tile([P, S], F32, name=f"a{v}")
+                    nc.scalar.copy(a_t[:], acc[:])
+                    a.append(a_t)
+
+        out_rows = out_0.rearrange("(p t) j -> p t j", t=PACK)
+        out_words = out_1[0].rearrange("p n t -> p (n t)").bitcast(I32)
+        o_codes = keep.tile([P, S], I32, align_bytes=64)
+        o_bytes = keep.tile([P, S], U8, align_bytes=64)
+
+        def planes(c0, c1, grouped):
+            nc.vector.quantize_mx(out=o_codes[:, c0:c1].bitcast(FP8X4), scales=o_bytes[:, c0:c1], in_=grouped)
+            nc.sync.dma_start(out_words[:, c0:c1], o_codes[:, c0:c1])
+
+        waiting = None
+        for c0, c1 in PIECES:
+            res = keep.tile([P, PACK, c1 - c0], F32, name=f"res{c0}")
+            for t in range(PACK):
+                nc.vector.tensor_tensor(res[:, t, :], a[t][:].indirect(entries(n5_sb, c0, c1)), prod[t][:, c0:c1], ALU.subtract)
+            if waiting:
+                planes(*waiting)
+            nc.sync.dma_start(out_rows[:, :, c0:c1], res[:])
+            waiting = (c0, c1, interleave(nc.vector.tensor_copy if c1 == S else nc.scalar.copy, res, f"grouped{c0}"))
+        planes(*waiting)
+        for q in range(4):
+            queue = nc.sync if q % 2 else nc.scalar
+            queue.dma_start(out_2[0][4 * q : 4 * q + 4, :].bitcast(I32), o_bytes[32 * q : 32 * q + 4, :].bitcast(I32))

@@ -82,6 +82,7 @@ def tile_picked_tiesoftbcmplift_none_po_kernel(
             nc.vector.quantize_mx(out=codes[:].bitcast(FP8X4), scales=scale_bytes[:], in_=grouped)
             return codes[:], scale_bytes[:]
 
+        w1w = load_words(w1_words, "w_words", nc.sync)
         xw = load_words(x_words, "xw", nc.sync)
         offs_sb = load_list(offs, "offs_sb")
         n3_sb = load_list(n3, "n3_sb")
@@ -89,9 +90,10 @@ def tile_picked_tiesoftbcmplift_none_po_kernel(
         n2_sb = load_list(n2, "n2_sb")
         n1_sb = load_list(n1, "n1_sb")
         n6_sb = load_list(n6, "n6_sb")
-        w1w = load_words(w1_words, "w1w", nc.sync)
         n5_sb = load_list(n5, "n5_sb")
-        xs = load_scales(x_scales, "xs", nc.gpsimd, [nc.scalar] * 4)
+        gain = keep.tile([P, PACK], F32)
+        nc.sync.dma_start(gain[:], gn.rearrange("(p t) o -> p (t o)", t=PACK))
+        xs = load_scales(x_scales, "xs", nc.vector, [nc.scalar] * 4)
         w1s = load_scales(w1_scales, "w1s", nc.gpsimd, [nc.gpsimd, nc.gpsimd, nc.scalar, nc.scalar])
         w2s = load_scales(w2_scales, "w2s", nc.vector, [nc.sync] * 4)
 
@@ -100,13 +102,11 @@ def tile_picked_tiesoftbcmplift_none_po_kernel(
         warm2 = keep.tile([P, 1], F32)
         nc.scalar.activation(warm2[:], warm[:], ACT.Sigmoid)
 
+        w1c = deal(w1w, I32, "w1c")
+        w2w = load_words(w2_words, "w_words", nc.sync)
         x_codes = keep.tile([P, S], U32, align_bytes=64)
         nc.vector.tensor_copy(x_codes[:], xw[:].bitcast(U32).indirect(offs_sb[:]))
-        w1c = deal(w1w, I32, "w1c")
-        w2w = load_words(w2_words, "w1w", nc.sync)
         w1b = deal(w1s, U8, "w1b")
-        gain = keep.tile([P, PACK], F32, name="w1s", align_bytes=64)
-        nc.sync.dma_start(gain[:], gn.rearrange("(p t) o -> p (t o)", t=PACK))
         x_bytes = keep.tile([P, S], U8, align_bytes=64)
         for c0 in (0, HALF):
             nc.vector.tensor_copy(x_bytes[:, c0 : c0 + HALF], xs[:].indirect(entries(offs_sb, c0, c0 + HALF)))
@@ -115,7 +115,8 @@ def tile_picked_tiesoftbcmplift_none_po_kernel(
 
         y = []
         for t in range(PACK):
-            y_t = keep.tile([P, S], F32, name=f"y{t}")
+            y_t = keep.tile([P, 2 * S], F32, name=f"y{t}")
+            nc.vector.memset(y_t[:, S:], 0.0)
             for c0 in (0, HALF):
                 acc = product(w1c, w1b, t, x_codes[:, c0 : c0 + HALF], x_bytes[:, c0 : c0 + HALF])
                 nc.scalar.copy(y_t[:, c0 : c0 + HALF], acc[:])
@@ -145,23 +146,18 @@ def tile_picked_tiesoftbcmplift_none_po_kernel(
         b_win = [keep.tile([P, 2 * S], F32, name=f"b_win{t}") for t in range(PACK)]
         y2, gate, tanh_b = {}, {}, []
         for s in range(PACK + 2):
-            for c0 in (0, HALF):
-                cols = slice(c0, c0 + HALF)
-                if s < PACK:
-                    if c0 == 0:
-                        y2[s] = ring.tile([P, S], F32, name="y2")
-                    nc.vector.tensor_copy(y2[s][:, cols], y[s][:].indirect(entries(n2_sb, c0, c0 + HALF)))
-                t = s - 1
-                if 0 <= t < PACK:
-                    nc.vector.tensor_tensor(
-                        b_win[t][:, S + c0 : S + c0 + HALF], y[t][:].indirect(entries(n1_sb, c0, c0 + HALF)), y2[t][:, cols], ALU.subtract
-                    )
+            t = s - 1
+            if s < PACK:
+                y2[s] = ring.tile([P, S], F32, name="y2")
+                nc.vector.tensor_copy(y2[s][:], y[s][:].indirect(n2_sb[:]))
+            if 0 <= t < PACK:
+                nc.vector.tensor_tensor(b_win[t][:, S:], y[t][:].indirect(n1_sb[:]), y2[t][:], ALU.subtract)
             if 0 <= t < PACK:
                 gate[t] = keep.tile([P, S], F32, name=f"gate{t % 2}")
                 nc.scalar.activation(gate[t][:], b_win[t][:, S:], ACT.Sigmoid)
             u = s - 2
             if u >= 0:
-                nc.vector.scalar_tensor_tensor(z_rows[:, u, :], gate[u][:], gain[:, u : u + 1], y[u][:], op0=ALU.mult, op1=ALU.mult)
+                nc.vector.scalar_tensor_tensor(z_rows[:, u, :], gate[u][:], gain[:, u : u + 1], y[u][:, :S], op0=ALU.mult, op1=ALU.mult)
             if s == 1:
                 z2_codes, z2_bytes = quantise(z2_grouped, "z2")
                 for v in range(PACK):

@@ -19,6 +19,7 @@ P = 128
 PACK = 4
 STRIPE = 16
 HALF = S // 2
+EARLY = 2
 PIECES = ((0, 256), (256, 384), (384, 512))
 
 
@@ -48,9 +49,9 @@ def tile_picked_tiesoftbcmplift_none_po_kernel(
                 queue.dma_start(tile[32 * q : 32 * q + 4, :].bitcast(I32), src[0][4 * q : 4 * q + 4, :].bitcast(I32))
             return tile
 
-        def deal(src, dtype, name):
+        def deal(src, dtype, name, engine):
             tile = keep.tile([P, H], dtype, name=name, align_bytes=64)
-            nc.vector.tensor_copy(tile[:].rearrange("p (t m) -> p t m", t=PACK), src[:].rearrange("p (m t) -> p t m", t=PACK))
+            engine.tensor_copy(tile[:].rearrange("p (t m) -> p t m", t=PACK), src[:].rearrange("p (m t) -> p t m", t=PACK))
             return tile
 
         def entries(lst, c0, c1):
@@ -79,7 +80,7 @@ def tile_picked_tiesoftbcmplift_none_po_kernel(
         def quantise(grouped, name):
             codes = keep.tile([P, S], U32, name=name + "_codes", align_bytes=64)
             scale_bytes = keep.tile([P, S], U8, name=name + "_bytes", align_bytes=64)
-            nc.vector.quantize_mx(out=codes[:].bitcast(FP8X4), scales=scale_bytes[:], in_=grouped)
+            nc.vector.quantize_mx(out=codes[:].bitcast(FP8X4), scales=scale_bytes[:], in_=grouped[:].rearrange("p c t -> p (c t)"))
             return codes[:], scale_bytes[:]
 
         w1w = load_words(w1_words, "w_words", nc.sync)
@@ -102,16 +103,16 @@ def tile_picked_tiesoftbcmplift_none_po_kernel(
         warm2 = keep.tile([P, 1], F32)
         nc.scalar.activation(warm2[:], warm[:], ACT.Sigmoid)
 
-        w1c = deal(w1w, I32, "w1c")
+        w1c = deal(w1w, I32, "w1c", nc.vector)
         w2w = load_words(w2_words, "w_words", nc.sync)
         x_codes = keep.tile([P, S], U32, align_bytes=64)
         nc.vector.tensor_copy(x_codes[:], xw[:].bitcast(U32).indirect(offs_sb[:]))
-        w1b = deal(w1s, U8, "w1b")
+        w1b = deal(w1s, U8, "w1b", nc.vector)
         x_bytes = keep.tile([P, S], U8, align_bytes=64)
         for c0 in (0, HALF):
             nc.vector.tensor_copy(x_bytes[:, c0 : c0 + HALF], xs[:].indirect(entries(offs_sb, c0, c0 + HALF)))
-        w2c = deal(w2w, I32, "w2c")
-        w2b = deal(w2s, U8, "w2b")
+        w2c = deal(w2w, I32, "w1s", nc.gpsimd)
+        w2b = deal(w2s, U8, "w2b", nc.gpsimd)
 
         y = []
         for t in range(PACK):
@@ -122,70 +123,95 @@ def tile_picked_tiesoftbcmplift_none_po_kernel(
                 nc.scalar.copy(y_t[:, c0 : c0 + HALF], acc[:])
             y.append(y_t)
 
-        z2_rows = keep.tile([P, PACK, S], BF16)
-        neg_pa, pb, rb, dt = {}, {}, {}, {}
-        for s in range(PACK + 1):
-            t, u = s, s - 1
-            if t < PACK:
-                neg_pa[t] = ring.tile([P, W], F32, name="neg_pa")
-                nc.vector.tensor_scalar(neg_pa[t][:], y[t][:].indirect(n3_sb[:]), -1.0, 0.0, op0=ALU.mult, op1=ALU.add)
-            if u >= 0:
-                rb[u] = ring.tile([P, W], F32, name="rb")
-                nc.vector.scalar_tensor_tensor(rb[u][:], neg_pa[u][:], -0.5, pb[u][:], op0=ALU.mult, op1=ALU.max)
-                dt[u] = ring.tile([P, S], F32, name="dt")
-                nc.vector.tensor_tensor(dt[u][:].indirect(n3_sb[:]), pb[u][:], neg_pa[u][:], ALU.add)
-            if t < PACK:
-                pb[t] = ring.tile([P, W], F32, name="pb")
-                nc.vector.tensor_copy(pb[t][:], y[t][:].indirect(n4_sb[:]))
-            if u >= 0:
-                nc.vector.tensor_copy(dt[u][:].indirect(n4_sb[:]), rb[u][:])
-                nc.scalar.activation(z2_rows[:, u, :], dt[u][:], ACT.Copy, scale=gain[:, u : u + 1])
-        z2_grouped = interleave(nc.scalar.copy, z2_rows, "z2_grouped")
-
+        z2_grouped = keep.tile([P, S, PACK], BF16, align_bytes=64)
+        z_grouped = keep.tile([P, S, PACK], BF16, align_bytes=64)
         z_rows = keep.tile([P, PACK, S], BF16)
         b_win = [keep.tile([P, 2 * S], F32, name=f"b_win{t}") for t in range(PACK)]
-        y2, gate, tanh_b = {}, {}, []
-        for s in range(PACK + 2):
-            t = s - 1
-            if s < PACK:
-                y2[s] = ring.tile([P, S], F32, name="y2")
-                nc.vector.tensor_copy(y2[s][:], y[s][:].indirect(n2_sb[:]))
-            if 0 <= t < PACK:
-                nc.vector.tensor_tensor(b_win[t][:, S:], y[t][:].indirect(n1_sb[:]), y2[t][:], ALU.subtract)
-            if 0 <= t < PACK:
-                gate[t] = keep.tile([P, S], F32, name=f"gate{t % 2}")
-                nc.scalar.activation(gate[t][:], b_win[t][:, S:], ACT.Sigmoid)
-            u = s - 2
-            if u >= 0:
-                nc.vector.scalar_tensor_tensor(z_rows[:, u, :], gate[u][:], gain[:, u : u + 1], y[u][:, :S], op0=ALU.mult, op1=ALU.mult)
-            if s == 1:
-                z2_codes, z2_bytes = quantise(z2_grouped, "z2")
-                for v in range(PACK):
-                    acc = product(w2c, w2b, v, z2_codes, z2_bytes)
-                    nc.scalar.copy(b_win[v][:, :S], acc[:])
-                    th_t = keep.tile([P, S], F32, name=f"tanh{v}")
-                    nc.scalar.activation(th_t[:], acc[:], ACT.Tanh)
-                    tanh_b.append(th_t)
-        z_grouped = interleave(nc.scalar.copy, z_rows, "z_grouped")
+        neg_pa, pb, y2, gate, tanh_b = {}, {}, {}, {}, []
 
-        prod = []
-        for t in range(PACK):
-            if t < 2:
-                p_t = keep.tile([P, S], F32, name=("y3", "gate1")[t])[:]
+        def fetch_pairs(t):
+            neg_pa[t] = ring.tile([P, W], F32, name="neg_pa")
+            nc.vector.tensor_scalar(neg_pa[t][:], y[t][:].indirect(n3_sb[:]), -1.0, 0.0, op0=ALU.mult, op1=ALU.add)
+            pb[t] = ring.tile([P, W], F32, name="pb")
+            nc.vector.tensor_copy(pb[t][:], y[t][:].indirect(n4_sb[:]))
+
+        def fetch_y2(t):
+            y2[t] = ring.tile([P, S], F32, name="y2")
+            nc.vector.tensor_copy(y2[t][:], y[t][:].indirect(n2_sb[:]))
+
+        def make_gate(t):
+            if t + 1 < PACK:
+                diff = ring.tile([P, S], F32, name="diff")
             else:
-                if t == 2:
-                    late = keep.tile([P, 2, S], F32, name="z_grouped", align_bytes=64)
-                p_t = late[:, t - 2, :]
+                diff = keep.tile([P, S], F32, name="z2_grouped", align_bytes=64)
+            nc.vector.tensor_tensor(diff[:], y[t][:].indirect(n1_sb[:]), y2[t][:], ALU.subtract)
+            gate[t] = b_win[t][:, S:]
+            nc.scalar.activation(gate[t], diff[:], ACT.Sigmoid)
+
+        def weave_pair(t):
+            nc.scalar.copy(
+                z_grouped[:].rearrange("p (c i) t -> p c t i", i=4)[:, :, t : t + 2, :],
+                z_rows[:, t : t + 2, :].rearrange("p t (c i) -> p c t i", i=4),
+            )
+
+        fetch_pairs(0)
+        fetch_y2(0)
+        for t in range(PACK):
+            rb = ring.tile([P, W], F32, name="rb")
+            nc.vector.scalar_tensor_tensor(rb[:], neg_pa[t][:], -0.5, pb[t][:], op0=ALU.mult, op1=ALU.max)
+            dt = keep.tile([P, S], F32, name=f"dt{t}")
+            nc.vector.tensor_tensor(dt[:].indirect(n3_sb[:]), pb[t][:], neg_pa[t][:], ALU.add)
+            if t < EARLY:
+                gained = ring.tile([P, S], F32, name="gained")
+                nc.scalar.activation(gained[:], y[t][:, :S], ACT.Copy, scale=gain[:, t : t + 1])
+                make_gate(t)
+                nc.gpsimd.tensor_tensor(z_rows[:, t, :], gate[t], gained[:], ALU.mult)
+            if t == EARLY:
+                weave_pair(0)
+            if t + 1 < PACK:
+                fetch_pairs(t + 1)
+            if t + 1 < EARLY or t + 1 == PACK:
+                fetch_y2(min(t + 1, EARLY))
+            nc.vector.tensor_copy(dt[:].indirect(n4_sb[:]), rb[:])
+            nc.scalar.activation(z2_grouped[:, :, t], dt[:], ACT.Copy, scale=gain[:, t : t + 1])
+
+        def gated(t):
+            nc.vector.scalar_tensor_tensor(z_rows[:, t, :], gate[t], gain[:, t : t + 1], y[t][:, :S], op0=ALU.mult, op1=ALU.mult)
+
+        def empty_b(t):
+            nc.scalar.copy(b_win[t][:, :S], b_acc[t][:])
+            th_t = keep.tile([P, S], F32, name=f"tanh{t}")
+            nc.scalar.activation(th_t[:], b_acc[t][:], ACT.Tanh)
+            tanh_b.append(th_t)
+
+        def tanh_product(t, p_t):
             nc.vector.tensor_tensor(p_t, b_win[t][:].indirect(n6_sb[:]), tanh_b[t][:], ALU.mult)
-            prod.append(p_t)
-            if t == 1:
-                z_codes, z_bytes = quantise(z_grouped, "z")
-                a = []
-                for v in range(PACK):
-                    acc = product(w2c, w2b, v, z_codes, z_bytes)
-                    a_t = keep.tile([P, S], F32, name=f"a{v}")
-                    nc.scalar.copy(a_t[:], acc[:])
-                    a.append(a_t)
+            return p_t
+
+        make_gate(2)
+        fetch_y2(3)
+        z2_codes, z2_bytes = quantise(z2_grouped, "z2")
+        make_gate(3)
+        b_acc = [product(w2c, w2b, t, z2_codes, z2_bytes) for t in range(PACK)]
+        gated(2)
+        gated(3)
+        empty_b(0)
+        empty_b(1)
+        weave_pair(2)
+        empty_b(2)
+        empty_b(3)
+
+        first_two = keep.tile([P, 2, S], F32, name="y3")
+        prod = [tanh_product(t, first_two[:, t, :]) for t in range(2)]
+        z_codes, z_bytes = quantise(z_grouped, "z")
+        a = []
+        for t in range(PACK):
+            acc = product(w2c, w2b, t, z_codes, z_bytes)
+            a_t = keep.tile([P, S], F32, name=f"a{t}")
+            nc.scalar.copy(a_t[:], acc[:])
+            a.append(a_t)
+        last_two = keep.tile([P, 2, S], F32, name="z_grouped", align_bytes=64)
+        prod.extend(tanh_product(2 + t, last_two[:, t, :]) for t in range(2))
 
         out_rows = out_0.rearrange("(p t) j -> p t j", t=PACK)
         out_words = out_1[0].rearrange("p n t -> p (n t)").bitcast(I32)

@@ -20,7 +20,6 @@ PACK = 4
 STRIPE = 16
 HALF = S // 2
 EARLY = 2
-PIECES = ((0, 256), (256, 384), (384, 512))
 
 
 def tile_picked_tiesoftbcmplift_none_po_kernel(
@@ -71,11 +70,8 @@ def tile_picked_tiesoftbcmplift_none_po_kernel(
             )
             return acc
 
-        def interleave(copy, rows, name):
-            width = rows.shape[2]
-            tile = keep.tile([P, width, PACK], BF16, name=name, align_bytes=64)
-            copy(tile[:].rearrange("p (c i) t -> p c t i", i=4), rows[:].rearrange("p t (c i) -> p c t i", i=4))
-            return tile[:].rearrange("p c t -> p (c t)")
+        def weave_pair(copy, grouped, pair, t):
+            copy(grouped[:].rearrange("p (c i) t -> p c t i", i=4)[:, :, t : t + 2, :], pair.rearrange("p t (c i) -> p c t i", i=4))
 
         def quantise(grouped, name):
             codes = keep.tile([P, S], U32, name=name + "_codes", align_bytes=64)
@@ -98,16 +94,11 @@ def tile_picked_tiesoftbcmplift_none_po_kernel(
         w1s = load_scales(w1_scales, "w1s", nc.gpsimd, [nc.gpsimd, nc.gpsimd, nc.scalar, nc.scalar])
         w2s = load_scales(w2_scales, "w2s", nc.vector, [nc.sync] * 4)
 
-        warm = keep.tile([P, 1], F32)
-        nc.vector.memset(warm[:], 0.0)
-        warm2 = keep.tile([P, 1], F32)
-        nc.scalar.activation(warm2[:], warm[:], ACT.Sigmoid)
-
         w1c = deal(w1w, I32, "w1c", nc.vector)
         w2w = load_words(w2_words, "w_words", nc.sync)
         x_codes = keep.tile([P, S], U32, align_bytes=64)
         nc.vector.tensor_copy(x_codes[:], xw[:].bitcast(U32).indirect(offs_sb[:]))
-        w1b = deal(w1s, U8, "w1b", nc.vector)
+        w1b = deal(w1s, U8, "w1b", nc.gpsimd)
         x_bytes = keep.tile([P, S], U8, align_bytes=64)
         for c0 in (0, HALF):
             nc.vector.tensor_copy(x_bytes[:, c0 : c0 + HALF], xs[:].indirect(entries(offs_sb, c0, c0 + HALF)))
@@ -118,9 +109,10 @@ def tile_picked_tiesoftbcmplift_none_po_kernel(
         for t in range(PACK):
             y_t = keep.tile([P, 2 * S], F32, name=f"y{t}")
             nc.vector.memset(y_t[:, S:], 0.0)
-            for c0 in (0, HALF):
-                acc = product(w1c, w1b, t, x_codes[:, c0 : c0 + HALF], x_bytes[:, c0 : c0 + HALF])
-                nc.scalar.copy(y_t[:, c0 : c0 + HALF], acc[:])
+            width = HALF if t == 0 else S
+            for c0 in range(0, S, width):
+                acc = product(w1c, w1b, t, x_codes[:, c0 : c0 + width], x_bytes[:, c0 : c0 + width])
+                nc.scalar.copy(y_t[:, c0 : c0 + width], acc[:])
             y.append(y_t)
 
         z2_grouped = keep.tile([P, S, PACK], BF16, align_bytes=64)
@@ -148,11 +140,6 @@ def tile_picked_tiesoftbcmplift_none_po_kernel(
             gate[t] = b_win[t][:, S:]
             nc.scalar.activation(gate[t], diff[:], ACT.Sigmoid)
 
-        def weave_pair(t):
-            nc.scalar.copy(
-                z_grouped[:].rearrange("p (c i) t -> p c t i", i=4)[:, :, t : t + 2, :],
-                z_rows[:, t : t + 2, :].rearrange("p t (c i) -> p c t i", i=4),
-            )
 
         fetch_pairs(0)
         fetch_y2(0)
@@ -167,7 +154,7 @@ def tile_picked_tiesoftbcmplift_none_po_kernel(
                 make_gate(t)
                 nc.gpsimd.tensor_tensor(z_rows[:, t, :], gate[t], gained[:], ALU.mult)
             if t == EARLY:
-                weave_pair(0)
+                weave_pair(nc.scalar.copy, z_grouped, z_rows[:, 0:2, :], 0)
             if t + 1 < PACK:
                 fetch_pairs(t + 1)
             if t + 1 < EARLY or t + 1 == PACK:
@@ -197,7 +184,7 @@ def tile_picked_tiesoftbcmplift_none_po_kernel(
         gated(3)
         empty_b(0)
         empty_b(1)
-        weave_pair(2)
+        weave_pair(nc.scalar.copy, z_grouped, z_rows[:, 2:4, :], 2)
         empty_b(2)
         empty_b(3)
 
@@ -218,20 +205,28 @@ def tile_picked_tiesoftbcmplift_none_po_kernel(
         o_codes = keep.tile([P, S], I32, align_bytes=64)
         o_bytes = keep.tile([P, S], U8, align_bytes=64)
 
-        def planes(c0, c1, grouped):
-            nc.vector.quantize_mx(out=o_codes[:, c0:c1].bitcast(FP8X4), scales=o_bytes[:, c0:c1], in_=grouped)
-            nc.sync.dma_start(out_words[:, c0:c1], o_codes[:, c0:c1])
+        def planes(c0, grouped):
+            cols = slice(c0, c0 + HALF)
+            nc.vector.quantize_mx(
+                out=o_codes[:, cols].bitcast(FP8X4), scales=o_bytes[:, cols], in_=grouped[:].rearrange("p c t -> p (c t)")
+            )
+            nc.sync.dma_start(out_words[:, cols], o_codes[:, cols])
 
-        waiting = None
-        for c0, c1 in PIECES:
-            res = keep.tile([P, PACK, c1 - c0], F32, name=f"res{c0}")
-            for t in range(PACK):
-                nc.vector.tensor_tensor(res[:, t, :], a[t][:].indirect(entries(n5_sb, c0, c1)), prod[t][:, c0:c1], ALU.subtract)
-            if waiting:
-                planes(*waiting)
-            nc.sync.dma_start(out_rows[:, :, c0:c1], res[:])
-            waiting = (c0, c1, interleave(nc.vector.tensor_copy if c1 == S else nc.scalar.copy, res, f"grouped{c0}"))
-        planes(*waiting)
+        grouped = {}
+        for c0 in (0, HALF):
+            grouped[c0] = keep.tile([P, HALF, PACK], BF16, name=f"grouped{c0}", align_bytes=64)
+            for t0 in (0, 2):
+                res = keep.tile([P, 2, HALF], F32, name=f"res{c0}_{t0}")
+                for t in (t0, t0 + 1):
+                    nc.vector.tensor_tensor(
+                        res[:, t - t0, :], a[t][:].indirect(entries(n5_sb, c0, c0 + HALF)), prod[t][:, c0 : c0 + HALF], ALU.subtract
+                    )
+                nc.sync.dma_start(out_rows[:, t0 : t0 + 2, c0 : c0 + HALF], res[:])
+                last = c0 == HALF and t0 == 2
+                if last:
+                    planes(0, grouped[0])
+                weave_pair(nc.vector.tensor_copy if last else nc.scalar.copy, grouped[c0], res[:], t0)
+        planes(HALF, grouped[HALF])
         for q in range(4):
             queue = nc.sync if q % 2 else nc.scalar
             queue.dma_start(out_2[0][4 * q : 4 * q + 4, :].bitcast(I32), o_bytes[32 * q : 32 * q + 4, :].bitcast(I32))

from contextlib import ExitStack

import concourse.mybir as mybir

K, T, S, H, W = 512, 2048, 512, 512, 256
FLOPS = 3 * 2 * K * H * S

F32 = mybir.dt.float32
BF16 = mybir.dt.bfloat16
I32 = mybir.dt.int32
U32 = mybir.dt.uint32
U16 = mybir.dt.uint16
U8 = mybir.dt.uint8
FP8X4 = mybir.dt.float8_e4m3fn_x4
ALU = mybir.AluOpType
ACT = mybir.ActivationFunctionType

P = 128
PACK = 4
STRIPE = 16
HALF = S // 2
EARLY = 2


def tile_picked_tiesoftbcmplift_none_po_kernel(
    tc, x_words, x_scales, w1_words, w1_scales, gn, w2_words, w2_scales, offs, n1, n2, n3, n4, n5, n6, out_0, out_1, out_2
):
    nc = tc.nc
    with ExitStack() as ctx:
        keep = ctx.enter_context(tc.tile_pool(name="keep", bufs=1))
        ring = ctx.enter_context(tc.tile_pool(name="ring", bufs=2))
        psum = ctx.enter_context(tc.psum_pool(name="psum", bufs=8))

        def load_list(src, name):
            tile = keep.tile(list(src.shape), U16, name=name)
            nc.sync.dma_start(tile[:], src)
            return tile

        def load_words(src, name, queue):
            tile = keep.tile([P, src.shape[2]], I32, name=name, align_bytes=64)
            queue.dma_start(tile[:], src[0].rearrange("p n t -> p (n t)").bitcast(I32))
            return tile

        def load_scales(src, name, clear, queues):
            tile = keep.tile([P, src.shape[2]], U8, name=name, align_bytes=64)
            clear.memset(tile[:].bitcast(I32), 0)
            for q, queue in enumerate(queues):
                queue.dma_start(tile[32 * q : 32 * q + 4, :].bitcast(I32), src[0][4 * q : 4 * q + 4, :].bitcast(I32))
            return tile

        def deal(src, dtype, name, engine):
            tile = keep.tile([P, H], dtype, name=name, align_bytes=64)
            engine.tensor_copy(tile[:].rearrange("p (t m) -> p t m", t=PACK), src[:].rearrange("p (m t) -> p t m", t=PACK))
            return tile

        def entries(lst, c0, c1):
            return lst[:, c0 // STRIPE : c1 // STRIPE]

        def product(w_codes, w_bytes, t, codes, scale_bytes):
            acc = psum.tile([P, codes.shape[1]], F32, name="acc")
            cols = slice(t * P, (t + 1) * P)
            nc.tensor.matmul_mx(
                out=acc[:],
                lhsT=w_codes[:, cols].bitcast(FP8X4),
                lhsT_scale=w_bytes[:, cols],
                rhs=codes.bitcast(FP8X4),
                rhs_scale=scale_bytes,
                start=True,
                stop=True,
            )
            return acc

        def weave_pair(copy, grouped, pair, t):
            copy(grouped[:].rearrange("p (c i) t -> p c t i", i=4)[:, :, t : t + 2, :], pair.rearrange("p t (c i) -> p c t i", i=4))

        def quantise(grouped, name):
            codes = keep.tile([P, S], U32, name=name + "_codes", align_bytes=64)
            scale_bytes = keep.tile([P, S], U8, name=name + "_bytes", align_bytes=64)
            nc.vector.quantize_mx(out=codes[:].bitcast(FP8X4), scales=scale_bytes[:], in_=grouped[:].rearrange("p c t -> p (c t)"))
            return codes[:], scale_bytes[:]

        w1w = load_words(w1_words, "w_words", nc.sync)
        xw = load_words(x_words, "xw", nc.sync)
        offs_sb = load_list(offs, "offs_sb")
        n3_sb = load_list(n3, "n3_sb")
        n4_sb = load_list(n4, "n4_sb")
        n2_sb = load_list(n2, "n2_sb")
        n1_sb = load_list(n1, "n1_sb")
        n6_sb = load_list(n6, "n6_sb")
        n5_sb = load_list(n5, "n5_sb")
        gain = keep.tile([P, PACK], F32)
        nc.sync.dma_start(gain[:], gn.rearrange("(p t) o -> p (t o)", t=PACK))
        xs = load_scales(x_scales, "xs", nc.vector, [nc.scalar] * 4)
        w1s = load_scales(w1_scales, "w1s", nc.gpsimd, [nc.gpsimd, nc.gpsimd, nc.scalar, nc.scalar])
        w2s = load_scales(w2_scales, "w2s", nc.vector, [nc.sync] * 4)

        w1c = deal(w1w, I32, "w1c", nc.vector)
        w2w = load_words(w2_words, "w_words", nc.sync)
        x_codes = keep.tile([P, S], U32, align_bytes=64)
        nc.vector.tensor_copy(x_codes[:], xw[:].bitcast(U32).indirect(offs_sb[:]))
        w1b = deal(w1s, U8, "w1b", nc.gpsimd)
        x_bytes = keep.tile([P, S], U8, align_bytes=64)
        for c0 in (0, HALF):
            nc.vector.tensor_copy(x_bytes[:, c0 : c0 + HALF], xs[:].indirect(entries(offs_sb, c0, c0 + HALF)))
        w2c = deal(w2w, I32, "w1s", nc.gpsimd)
        w2b = deal(w2s, U8, "w2b", nc.gpsimd)

        y = []
        for t in range(PACK):
            y_t = keep.tile([P, 2 * S], F32, name=f"y{t}")
            nc.vector.memset(y_t[:, S:], 0.0)
            width = HALF if t == 0 else S
            for c0 in range(0, S, width):
                acc = product(w1c, w1b, t, x_codes[:, c0 : c0 + width], x_bytes[:, c0 : c0 + width])
                nc.scalar.copy(y_t[:, c0 : c0 + width], acc[:])
            y.append(y_t)

        z2_grouped = keep.tile([P, S, PACK], BF16, align_bytes=64)
        z_grouped = keep.tile([P, S, PACK], BF16, align_bytes=64)
        z_rows = keep.tile([P, PACK, S], BF16)
        b_win = [keep.tile([P, 2 * S], F32, name=f"b_win{t}") for t in range(PACK)]
        neg_pa, pb, y2, gate, tanh_b = {}, {}, {}, {}, []

        def fetch_pairs(t):
            neg_pa[t] = ring.tile([P, W], F32, name="neg_pa")
            nc.vector.tensor_scalar(neg_pa[t][:], y[t][:].indirect(n3_sb[:]), -1.0, 0.0, op0=ALU.mult, op1=ALU.add)
            pb[t] = ring.tile([P, W], F32, name="pb")
            nc.vector.tensor_copy(pb[t][:], y[t][:].indirect(n4_sb[:]))

        def fetch_y2(t):
            y2[t] = ring.tile([P, S], F32, name="y2")
            nc.vector.tensor_copy(y2[t][:], y[t][:].indirect(n2_sb[:]))

        def make_gate(t):
            if t + 1 < PACK:
                diff = ring.tile([P, S], F32, name="diff")
            else:
                diff = keep.tile([P, S], F32, name="z2_grouped", align_bytes=64)
            nc.vector.tensor_tensor(diff[:], y[t][:].indirect(n1_sb[:]), y2[t][:], ALU.subtract)
            gate[t] = b_win[t][:, S:]
            nc.scalar.activation(gate[t], diff[:], ACT.Sigmoid)


        fetch_pairs(0)
        fetch_y2(0)
        for t in range(PACK):
            rb = ring.tile([P, W], F32, name="rb")
            nc.vector.scalar_tensor_tensor(rb[:], neg_pa[t][:], -0.5, pb[t][:], op0=ALU.mult, op1=ALU.max)
            dt = keep.tile([P, S], F32, name=f"dt{t}")
            nc.vector.tensor_tensor(dt[:].indirect(n3_sb[:]), pb[t][:], neg_pa[t][:], ALU.add)
            if t < EARLY:
                gained = ring.tile([P, S], F32, name="gained")
                nc.scalar.activation(gained[:], y[t][:, :S], ACT.Copy, scale=gain[:, t : t + 1])
                make_gate(t)
                nc.gpsimd.tensor_tensor(z_rows[:, t, :], gate[t], gained[:], ALU.mult)
            if t == EARLY:
                weave_pair(nc.scalar.copy, z_grouped, z_rows[:, 0:2, :], 0)
            if t + 1 < PACK:
                fetch_pairs(t + 1)
            if t + 1 < EARLY or t + 1 == PACK:
                fetch_y2(min(t + 1, EARLY))
            nc.vector.tensor_copy(dt[:].indirect(n4_sb[:]), rb[:])
            nc.scalar.activation(z2_grouped[:, :, t], dt[:], ACT.Copy, scale=gain[:, t : t + 1])

        def gated(t):
            nc.vector.scalar_tensor_tensor(z_rows[:, t, :], gate[t], gain[:, t : t + 1], y[t][:, :S], op0=ALU.mult, op1=ALU.mult)

        def empty_b(t):
            nc.scalar.copy(b_win[t][:, :S], b_acc[t][:])
            th_t = keep.tile([P, S], F32, name=f"tanh{t}")
            nc.scalar.activation(th_t[:], b_acc[t][:], ACT.Tanh)
            tanh_b.append(th_t)

        def tanh_product(t, p_t):
            nc.vector.tensor_tensor(p_t, b_win[t][:].indirect(n6_sb[:]), tanh_b[t][:], ALU.mult)
            return p_t

        make_gate(2)
        fetch_y2(3)
        z2_codes, z2_bytes = quantise(z2_grouped, "z2")
        make_gate(3)
        b_acc = [product(w2c, w2b, t, z2_codes, z2_bytes) for t in range(PACK)]
        gated(2)
        gated(3)
        empty_b(0)
        empty_b(1)
        weave_pair(nc.scalar.copy, z_grouped, z_rows[:, 2:4, :], 2)
        empty_b(2)
        empty_b(3)

        first_two = keep.tile([P, 2, S], F32, name="y3")
        prod = [tanh_product(t, first_two[:, t, :]) for t in range(2)]
        z_codes, z_bytes = quantise(z_grouped, "z")
        a = []
        for t in range(PACK):
            acc = product(w2c, w2b, t, z_codes, z_bytes)
            a_t = keep.tile([P, S], F32, name=f"a{t}")
            nc.scalar.copy(a_t[:], acc[:])
            a.append(a_t)
        last_two = keep.tile([P, 2, S], F32, name="z_grouped", align_bytes=64)
        prod.extend(tanh_product(2 + t, last_two[:, t, :]) for t in range(2))

        out_rows = out_0.rearrange("(p t) j -> p t j", t=PACK)
        out_words = out_1[0].rearrange("p n t -> p (n t)").bitcast(I32)
        o_codes = keep.tile([P, S], I32, align_bytes=64)
        o_bytes = keep.tile([P, S], U8, align_bytes=64)

        def planes(c0, grouped):
            cols = slice(c0, c0 + HALF)
            nc.vector.quantize_mx(
                out=o_codes[:, cols].bitcast(FP8X4), scales=o_bytes[:, cols], in_=grouped[:].rearrange("p c t -> p (c t)")
            )
            nc.sync.dma_start(out_words[:, cols], o_codes[:, cols])

        grouped = {}
        for c0 in (0, HALF):
            grouped[c0] = keep.tile([P, HALF, PACK], BF16, name=f"grouped{c0}", align_bytes=64)
            for t0 in (0, 2):
                res = keep.tile([P, 2, HALF], F32, name=f"res{c0}_{t0}")
                for t in (t0, t0 + 1):
                    nc.vector.tensor_tensor(
                        res[:, t - t0, :], a[t][:].indirect(entries(n5_sb, c0, c0 + HALF)), prod[t][:, c0 : c0 + HALF], ALU.subtract
                    )
                nc.sync.dma_start(out_rows[:, t0 : t0 + 2, c0 : c0 + HALF], res[:])
                last = c0 == HALF and t0 == 2
                if last:
                    planes(0, grouped[0])
                weave_pair(nc.vector.tensor_copy if last else nc.scalar.copy, grouped[c0], res[:], t0)
        planes(HALF, grouped[HALF])
        for q in range(4):
            queue = nc.sync if q % 2 else nc.scalar
            queue.dma_start(out_2[0][4 * q : 4 * q + 4, :].bitcast(I32), o_bytes[32 * q : 32 * q + 4, :].bitcast(I32))
